import numpy as np
import ml_dtypes


def mxq(x, axis, fmt="e4m3"):
    dtype, down = {"e4m3": (ml_dtypes.float8_e4m3fn, 7), "e5m2": (ml_dtypes.float8_e5m2, 14)}[fmt]
    v = np.moveaxis(np.asarray(x, np.float32).astype(ml_dtypes.bfloat16).astype(np.float64), axis, -1)
    blocks = v.reshape(v.shape[:-1] + (-1, 32))
    amax = np.abs(blocks).max(-1, keepdims=True)
    byte = np.maximum(np.where(amax > 0, np.frexp(amax)[1] - 1 + 127, 0) - down, 1)
    scale = np.exp2(byte - 127.0)
    codes = (blocks / scale).astype(np.float32).astype(dtype).astype(np.float64)
    return np.moveaxis((codes * scale).reshape(v.shape), -1, axis)


WIDE = False


def mx_kscale(k):
    if not WIDE:
        return np.ones(k)
    levels = np.array([10, -10, 5, -5, 0])
    if k % 512:
        return np.exp2(np.random.permutation(np.resize(levels, k // 32))).repeat(32)
    a = np.empty((k // 512, 16))
    for p in range(k // 512):
        a[p, :8] = np.random.permutation(np.resize(levels, 8))
        for g in range(8):
            far = levels[np.abs(levels - a[p, g]) >= 10]
            a[p, g + 8] = far[np.random.randint(len(far))]
    return np.exp2(a.ravel()).repeat(32)


def f64(x):
    return np.asarray(x).astype(np.float64)


def striped(idx):
    return np.tile(idx.reshape(-1, 16).T, (8, 1)).astype(np.uint16)


def unstriped(offs):
    return offs[:16].T.reshape(-1).astype(np.int64)


def striped8(idx):
    return np.concatenate([x.reshape(-1, 16).T for x in idx]).astype(np.uint16)


def runs(offs, k):
    lists = np.stack([offs[16 * r : 16 * r + 16].T.reshape(-1) for r in range(8)]).astype(np.int64)
    return lists[np.arange(k) % 512 // 64]


def pack_weight(w):
    k, n = w.shape
    w = f64(np.asarray(w, np.float32).astype(ml_dtypes.bfloat16)).reshape(k // 32, 32, n)
    amax = np.abs(w).max(1)
    byte = np.clip(np.where(amax > 0, np.frexp(amax)[1] - 1 + 127 - 7, 1), 1, 254)
    scaled = (w * np.exp2(127.0 - byte)[:, None, :]).reshape(k, n).astype(np.float32)
    words = np.ascontiguousarray(scaled.reshape(k // 512, 128, 4, n).transpose(0, 1, 3, 2)).astype(ml_dtypes.float8_e4m3fn).view(np.uint8)
    return words, np.ascontiguousarray(byte.astype(np.uint8).reshape(k // 512, 16, n))


def unpack_weight(words, scales):
    g, p, n, _ = words.shape
    vals = np.ascontiguousarray(words).view(ml_dtypes.float8_e4m3fn).astype(np.float64) * np.repeat(np.exp2(scales.astype(np.float64) - 127.0), 8, axis=1)[..., None]
    return vals.transpose(0, 1, 3, 2).reshape(g * 512, n)


K, T, S, H, C = 512, 2048, 512, 512, 512


def setup_inputs():
    n = np.random.standard_normal
    s = mx_kscale(K)[:, None]
    packed_xT = pack_weight(n((K, T)) * s)
    return {
        "x_words": packed_xT[0],
        "x_scales": packed_xT[1],
        "w1": (n((K, H)) / np.sqrt(K) / s).astype(np.float32),
        "w2": (n((K, H)) / np.sqrt(K) / s).astype(np.float32),
        "gs": (np.random.uniform(0.5, 1.5, (K, 1)) / s).astype(np.float32),
        "offs": striped(np.random.permutation(T)[:S]),
        "two": striped(np.random.permutation(T)[:S]),
        "n1": striped8(np.stack([np.random.permutation(S) for _ in range(8)])),
        "n2": striped8(np.stack([np.random.permutation(S) for _ in range(8)])),
        "n3": striped8(np.stack([np.random.permutation(S) for _ in range(8)])),
        "n4": striped8(np.stack([np.random.permutation(S) for _ in range(8)])),
        "cand": striped(np.random.permutation(T)[:C]),
        "n5": striped8(np.stack([np.random.permutation(S) for _ in range(8)])),
        "n6": striped8(np.stack([np.random.permutation(S) for _ in range(8)])),
    }


def reference(x_words, x_scales, w1, w2, gs, offs, two, n1, n2, n3, n4, cand, n5, n6):
    x_cand = unpack_weight(x_words, x_scales)[:, unstriped(cand)]
    xq = unpack_weight(x_words, x_scales)[:, unstriped(offs)]
    y = mxq(f64(w1), 0, "e4m3").T @ xq
    x_two = unpack_weight(x_words, x_scales)[:, unstriped(two)]
    d = mxq(f64(w2), 0, "e4m3").T @ x_two
    z = f64(gs) * (np.maximum(y[np.arange(H)[:, None], runs(n1, H)] + d[np.arange(H)[:, None], runs(n3, H)], y[np.arange(H)[:, None], runs(n2, H)] + d[np.arange(H)[:, None], runs(n4, H)]))
    s = 0.0625 * ((x_cand.T @ mxq(z, 0, "e4m3")))
    pa = s[np.arange(C)[:, None], runs(n5, C)]
    pb = s[np.arange(C)[:, None], runs(n6, C)]
    mu = 0.3125 * (s + pa + pb)
    return (s - mu) / (np.sqrt((pa - mu) ** 2 + (pb - mu) ** 2 + 0.25))

@@ -1,0 +1,192 @@
+from contextlib import ExitStack
+import math
+
+import concourse.mybir as mybir
+from concourse.masks import make_identity
+
+K, T, S = 512, 2048, 512
+FLOPS = 3 * 2 * 512 * 512 * 512
+
+F32 = mybir.dt.float32
+BF16 = mybir.dt.bfloat16
+I32 = mybir.dt.int32
+U32 = mybir.dt.uint32
+U16 = mybir.dt.uint16
+U8 = mybir.dt.uint8
+FP8X4 = mybir.dt.float8_e4m3fn_x4
+ACT = mybir.ActivationFunctionType
+ALU = mybir.AluOpType
+
+P = 128
+PACK = 4
+HALF = S // 2
+
+
+def tile_picked_twcpathbstd_none_p_kernel(tc, x_words, x_scales, w1, w2, gs, offs, two, n1, n2, n3, n4, cand, n5, n6, out):
+    nc = tc.nc
+    with ExitStack() as ctx:
+        lists = ctx.enter_context(tc.tile_pool(name="lists", bufs=1))
+        keep = ctx.enter_context(tc.tile_pool(name="keep", bufs=1))
+        work = ctx.enter_context(tc.tile_pool(name="work", bufs=2))
+        psum = ctx.enter_context(tc.psum_pool(name="psum", bufs=1))
+
+        def load_list(name, src):
+            t = lists.tile([P, S // 16], U16, name=name)
+            nc.sync.dma_start(t[:], src)
+            return t
+
+        def load_half(name, w, h):
+            raw = keep.tile([P, PACK, HALF], F32, name=name)
+            nc.sync.dma_start(raw[:], w.rearrange("(p j) c -> p j c", j=PACK)[:, :, HALF * h : HALF * (h + 1)])
+            return raw
+
+        xs = keep.tile([P, T], U8, name="xs", align_bytes=64)
+        nc.vector.memset(xs[:].bitcast(I32), 0)
+        for q in range(4):
+            nc.scalar.dma_start(xs[32 * q : 32 * q + 4, :].bitcast(I32), x_scales[0, 4 * q : 4 * q + 4, :].bitcast(I32))
+        l_offs = load_list("l_offs", offs)
+        l_two = load_list("l_two", two)
+        raw1 = [load_half("raw1%d" % h, w1, h) for h in range(2)]
+        l_cand = load_list("l_cand", cand)
+        xw = keep.tile([P, T], U32, name="xw", align_bytes=64)
+        nc.sync.dma_start(xw[:].bitcast(I32), x_words[0].rearrange("p n t -> p (n t)").bitcast(I32))
+        raw2 = [load_half("raw2%d" % h, w2, h) for h in range(2)]
+        l_n1 = load_list("l_n1", n1)
+        l_n2 = load_list("l_n2", n2)
+        l_n3 = load_list("l_n3", n3)
+        l_n4 = load_list("l_n4", n4)
+        gs_t = keep.tile([P, PACK], F32, name="gs_t")
+        nc.sync.dma_start(gs_t[:], gs.rearrange("(p t) o -> p (t o)", t=PACK))
+        l_n5 = load_list("l_n5", n5)
+        l_n6 = load_list("l_n6", n6)
+
+        wins = []
+        for i in range(4):
+            win = keep.tile([P, 2 * S], F32, name="win%d" % i)
+            nc.vector.memset(win[:, S:], 0.0)
+            wins.append(win)
+        ident = keep.tile([P, P], F32, name="ident")
+        make_identity(nc, ident[:])
+
+        def bank(i):
+            return psum.tile([P, S], F32, name="bank%d" % i)
+
+        def turn(dst, srcs, n):
+            for c in range(n // P):
+                cols = slice(P * c, P * (c + 1))
+                for i, src in enumerate(srcs):
+                    nc.tensor.matmul(dst[:, cols], src[:, cols], ident[:], start=(i == 0), stop=(i == len(srcs) - 1), is_transpose=True)
+
+        def pick(name, table, dtype, lst):
+            got = keep.tile([P, S], dtype, name=name, align_bytes=64)
+            nc.vector.tensor_copy(got[:], table[:].indirect(lst[:]))
+            return got
+
+        def weave(wg, raw, h):
+            v = wg[:].rearrange("p (t m j) -> p m t j", t=PACK, j=PACK)
+            nc.scalar.copy(v[:, 64 * h : 64 * (h + 1)], raw[:].rearrange("p j (m t) -> p m t j", t=PACK))
+
+        def codes(name):
+            return (keep.tile([P, S], U32, name=name + "_c", align_bytes=64), keep.tile([P, S], U8, name=name + "_p", align_bytes=64))
+
+        def quant(dst, src, cols=slice(0, S)):
+            nc.vector.quantize_mx(out=dst[0][:, cols].bitcast(FP8X4), scales=dst[1][:, cols], in_=src[:])
+
+        def mm(dst, lhs, t, rhs, cols=slice(0, S)):
+            m = slice(P * t, P * (t + 1))
+            nc.tensor.matmul_mx(out=dst, lhsT=lhs[0][:, m].bitcast(FP8X4), lhsT_scale=lhs[1][:, m], rhs=rhs[0][:, cols].bitcast(FP8X4), rhs_scale=rhs[1][:, cols], start=True, stop=True)
+
+        offs_s = pick("offs_s", xs, U8, l_offs)
+        two_s = pick("two_s", xs, U8, l_two)
+        cand_s = pick("cand_s", xs, U8, l_cand)
+        wg1 = keep.tile([P, PACK * S], BF16, name="wg1", align_bytes=64)
+        wg2 = keep.tile([P, PACK * S], BF16, name="wg2", align_bytes=64)
+        weave(wg1, raw1[0], 0)
+        weave(wg1, raw1[1], 1)
+        w1q = codes("w1")
+        quant(w1q, wg1)
+        xq = (pick("offs_w", xw, U32, l_offs), offs_s)
+        xt = (pick("two_w", xw, U32, l_two), two_s)
+        cand_sd = keep.tile([P, S], U8, name="cand_sd", align_bytes=64)
+        nc.vector.tensor_copy(cand_sd[:].rearrange("p (t m) -> p m t", t=PACK), cand_s[:].rearrange("p (m t) -> p m t", t=PACK))
+        w2q = codes("w2")
+
+        zg = [keep.tile([P, PACK * HALF], BF16, name="zg%d" % h, align_bytes=64) for h in range(2)]
+        for t in range(PACK):
+            by, bd = bank(t % 2), bank(2 + t % 2)
+            yw, dw = wins[2 * (t % 2)], wins[2 * (t % 2) + 1]
+            if t == 0:
+                weave(wg2, raw2[0], 0)
+            mm(by[:], w1q, t, xq)
+            nc.scalar.copy(yw[:, :S], by[:])
+            if t == 1:
+                g1 = keep.tile([P, S], F32, name="wg2", align_bytes=64)
+            else:
+                g1 = work.tile([P, S], F32, name="g1")
+            g2 = work.tile([P, S], F32, name="g2")
+            if t < PACK - 1:
+                a = work.tile([P, S], F32, name="a")
+            else:
+                a = keep.tile([P, S], F32, name="late", align_bytes=64)
+            b = work.tile([P, S], F32, name="b")
+            m = work.tile([P, S], F32, name="m")
+            nc.vector.tensor_copy(g1[:], yw[:].indirect(l_n1[:]))
+            nc.vector.tensor_copy(g2[:], yw[:].indirect(l_n2[:]))
+            if t == 0:
+                weave(wg2, raw2[1], 1)
+                quant(w2q, wg2)
+            mm(bd[:], w2q, t, xt)
+            nc.scalar.copy(dw[:, :S], bd[:])
+            nc.vector.tensor_tensor(a[:], dw[:].indirect(l_n3[:]), g1[:], ALU.add)
+            nc.vector.tensor_tensor(b[:], dw[:].indirect(l_n4[:]), g2[:], ALU.add)
+            nc.vector.tensor_tensor(m[:], a[:], b[:], ALU.max)
+            for h in range(2):
+                nc.scalar.activation(zg[h][:].rearrange("p (n t) -> p t n", t=PACK)[:, t, :], m[:, HALF * h : HALF * (h + 1)], ACT.Copy, scale=gs_t[:, t : t + 1])
+
+        cand_w = pick("late", xw, U32, l_cand)
+        cand_wd = keep.tile([P, S], U32, name="cand_wd", align_bytes=64)
+        nc.vector.tensor_copy(cand_wd[:].rearrange("p (t c i) -> p c t i", t=PACK, i=4), cand_w[:].rearrange("p (c i t) -> p c t i", t=PACK, i=4))
+        xc = (cand_wd, cand_sd)
+        zq = codes("z")
+        for h in range(2):
+            quant(zq, zg[h], slice(HALF * h, HALF * (h + 1)))
+
+        ov = out.rearrange("(p t) n -> t p n", t=PACK)
+        nxs = [keep.tile([P, S], F32, name="nx%d" % t) for t in range(PACK)]
+        for h in range(2):
+            cols = slice(HALF * h, HALF * (h + 1))
+            bs = bank(h)
+            mm(bs[:, :HALF], xc, 0, zq, cols)
+            nc.scalar.activation(wins[0][:, cols], bs[:, :HALF], ACT.Copy, scale=0.0625)
+        nc.scalar.activation(nxs[0][:], wins[0][:, :S], ACT.Copy, scale=-5.0 / 3.0)
+        for t in range(1, PACK):
+            bs = bank(t % 2)
+            mm(bs[:], xc, t, zq)
+            nc.scalar.activation(wins[t][:, :S], bs[:], ACT.Copy, scale=0.0625)
+            nc.scalar.activation(nxs[t][:], bs[:], ACT.Copy, scale=-0.0625 * 5.0 / 3.0)
+        pieces = [(t, 0, S) for t in range(PACK - 1)] + [(PACK - 1, 0, HALF), (PACK - 1, HALF, S)]
+        for k, (t, c0, c1) in enumerate(pieces):
+            sp, nx = wins[t], nxs[t]
+            n = c1 - c0
+            lc = slice(c0 // 16, c1 // 16)
+            v = work.tile([P, n], F32, name="g1")
+            ws = work.tile([P, n], F32, name="g2")
+            e = work.tile([P, n], F32, name="a")
+            nn = work.tile([P, n], F32, name="nn", bufs=4)
+            sq1 = work.tile([P, n], F32, name="sq1")
+            sq2 = work.tile([P, n], F32, name="sq2")
+            r = work.tile([P, n], F32, name="r")
+            o = work.tile([P, n], F32, name="o", bufs=4)
+            be, bp, bq = bank(2 + k % 2), bank(4 + k % 2), bank(6 + k % 2)
+            nc.vector.tensor_copy(v[:], sp[:].indirect(l_n6[:, lc]))
+            nc.vector.tensor_tensor(ws[:], sp[:].indirect(l_n5[:, lc]), v[:], ALU.add)
+            turn(bp, (nx[:, c0:c1], ws), n)
+            nc.scalar.activation(sq2[:], bp[:, :n], ACT.Square, scale=0.375 * math.sqrt(0.5))
+            nc.vector.scalar_tensor_tensor(e[:], v[:], -2.0, ws[:], ALU.mult, ALU.add)
+            turn(be, (e,), n)
+            nc.scalar.activation(sq1[:], be[:, :n], ACT.Square, scale=math.sqrt(0.5))
+            nc.vector.scalar_tensor_tensor(nn[:], sp[:, c0:c1], -2.2, ws[:], ALU.mult, ALU.add)
+            turn(bq, (sq2, sq1), n)
+            nc.scalar.activation(r[:], bq[:, :n], ACT.Abs_reciprocal_sqrt, bias=0.25)
+            nc.vector.scalar_tensor_tensor(o[:], nn[:], -0.3125, r[:], ALU.mult, ALU.mult)
+            nc.sync.dma_start(ov[t][:, c0:c1], o[:])

@@ -1,11 +1,12 @@
-from contextlib import ExitStack
 import math
+from contextlib import ExitStack
 
 import concourse.mybir as mybir
 from concourse.masks import make_identity
 
-K, T, S = 512, 2048, 512
-FLOPS = 3 * 2 * 512 * 512 * 512
+T = 2048
+S = 512
+FLOPS = 3 * 2 * S * S * S
 
 F32 = mybir.dt.float32
 BF16 = mybir.dt.bfloat16
@@ -20,6 +21,12 @@ ALU = mybir.AluOpType
 P = 128
 PACK = 4
 HALF = S // 2
+ALIGN = 64
+WINDOWS = 6
+LAST = PACK - 1
+
+S_SCALE = 0.0625
+MU = 0.3125
 
 
 def tile_picked_twcpathbstd_none_p_kernel(tc, x_words, x_scales, w1, w2, gs, offs, two, n1, n2, n3, n4, cand, n5, n6, out):
@@ -31,162 +38,217 @@ def tile_picked_twcpathbstd_none_p_kernel(tc, x_words, x_scales, w1, w2, gs, off
         psum = ctx.enter_context(tc.psum_pool(name="psum", bufs=1))
 
         def load_list(name, src):
-            t = lists.tile([P, S // 16], U16, name=name)
-            nc.sync.dma_start(t[:], src)
-            return t
+            loaded = lists.tile([P, S // 16], U16, name=name)
+            nc.sync.dma_start(loaded[:], src)
+            return loaded
 
-        def load_half(name, w, h):
+        def load_half(name, weight, h):
             raw = keep.tile([P, PACK, HALF], F32, name=name)
-            nc.sync.dma_start(raw[:], w.rearrange("(p j) c -> p j c", j=PACK)[:, :, HALF * h : HALF * (h + 1)])
+            nc.sync.dma_start(raw[:], weight.rearrange("(p j) c -> p j c", j=PACK)[:, :, HALF * h : HALF * (h + 1)])
             return raw
 
-        xs = keep.tile([P, T], U8, name="xs", align_bytes=64)
-        nc.vector.memset(xs[:].bitcast(I32), 0)
-        for q in range(4):
-            nc.scalar.dma_start(xs[32 * q : 32 * q + 4, :].bitcast(I32), x_scales[0, 4 * q : 4 * q + 4, :].bitcast(I32))
+        x_bytes = keep.tile([P, T], U8, name="x_bytes", align_bytes=ALIGN)
+        nc.vector.memset(x_bytes[:, : T // 2].bitcast(I32), 0)
+        nc.gpsimd.memset(x_bytes[:, T // 2 :].bitcast(I32), 0)
+        sixteen = keep.tile([P, 1], F32, name="sixteen")
+        nc.vector.memset(sixteen[:], 16.0)
+
         l_offs = load_list("l_offs", offs)
         l_two = load_list("l_two", two)
-        raw1 = [load_half("raw1%d" % h, w1, h) for h in range(2)]
+        x_codes = keep.tile([P, T], U32, name="x_codes", align_bytes=ALIGN)
+        nc.sync.dma_start(x_codes[:].bitcast(I32), x_words[0].rearrange("p n t -> p (n t)").bitcast(I32))
+        raw1 = [load_half("raw10", w1, 0)]
+        for q in range(4):
+            nc.sync.dma_start(x_bytes[32 * q : 32 * q + 4, :].bitcast(I32), x_scales[0, 4 * q : 4 * q + 4, :].bitcast(I32))
+        raw1.append(load_half("raw11", w1, 1))
         l_cand = load_list("l_cand", cand)
-        xw = keep.tile([P, T], U32, name="xw", align_bytes=64)
-        nc.sync.dma_start(xw[:].bitcast(I32), x_words[0].rearrange("p n t -> p (n t)").bitcast(I32))
         raw2 = [load_half("raw2%d" % h, w2, h) for h in range(2)]
         l_n1 = load_list("l_n1", n1)
         l_n2 = load_list("l_n2", n2)
         l_n3 = load_list("l_n3", n3)
         l_n4 = load_list("l_n4", n4)
-        gs_t = keep.tile([P, PACK], F32, name="gs_t")
-        nc.sync.dma_start(gs_t[:], gs.rearrange("(p t) o -> p (t o)", t=PACK))
+        gains = keep.tile([P, PACK], F32, name="gains")
+        nc.sync.dma_start(gains[:], gs.rearrange("(p t) o -> p (t o)", t=PACK))
         l_n5 = load_list("l_n5", n5)
         l_n6 = load_list("l_n6", n6)
 
-        wins = []
-        for i in range(4):
-            win = keep.tile([P, 2 * S], F32, name="win%d" % i)
-            nc.vector.memset(win[:, S:], 0.0)
-            wins.append(win)
+        windows = []
+        for i in range(WINDOWS):
+            window = keep.tile([P, 2 * S], F32, name="window%d" % i)
+            nc.vector.memset(window[:, S:], 0.0)
+            windows.append(window)
+        quarter = keep.tile([P, 1], F32, name="quarter")
+        nc.scalar.activation(quarter[:], sixteen[:], ACT.Abs_reciprocal_sqrt)
         ident = keep.tile([P, P], F32, name="ident")
         make_identity(nc, ident[:])
 
         def bank(i):
             return psum.tile([P, S], F32, name="bank%d" % i)
 
-        def turn(dst, srcs, n):
-            for c in range(n // P):
-                cols = slice(P * c, P * (c + 1))
-                for i, src in enumerate(srcs):
-                    nc.tensor.matmul(dst[:, cols], src[:, cols], ident[:], start=(i == 0), stop=(i == len(srcs) - 1), is_transpose=True)
+        def turn_and_add(dst, sources, width):
+            for c in range(width // P):
+                block = slice(P * c, P * (c + 1))
+                for i, src in enumerate(sources):
+                    nc.tensor.matmul(dst[:, block], src[:, block], ident[:], start=(i == 0), stop=(i == len(sources) - 1), is_transpose=True)
 
-        def pick(name, table, dtype, lst):
-            got = keep.tile([P, S], dtype, name=name, align_bytes=64)
-            nc.vector.tensor_copy(got[:], table[:].indirect(lst[:]))
-            return got
+        def pick(tag, table, dtype, offsets):
+            picked = keep.tile([P, S], dtype, name=tag, align_bytes=ALIGN)
+            nc.vector.tensor_copy(picked[:], table[:].indirect(offsets[:]))
+            return picked
 
-        def weave(wg, raw, h):
-            v = wg[:].rearrange("p (t m j) -> p m t j", t=PACK, j=PACK)
-            nc.scalar.copy(v[:, 64 * h : 64 * (h + 1)], raw[:].rearrange("p j (m t) -> p m t j", t=PACK))
+        def weave(woven, raw, h):
+            dealt = woven[:].rearrange("p (t m j) -> p m t j", t=PACK, j=PACK)
+            per_half = HALF // PACK
+            nc.scalar.copy(dealt[:, per_half * h : per_half * (h + 1)], raw[:].rearrange("p j (m t) -> p m t j", t=PACK))
 
-        def codes(name):
-            return (keep.tile([P, S], U32, name=name + "_c", align_bytes=64), keep.tile([P, S], U8, name=name + "_p", align_bytes=64))
+        def mx_operand(name):
+            return (keep.tile([P, S], U32, name=name + "_codes", align_bytes=ALIGN), keep.tile([P, S], U8, name=name + "_bytes", align_bytes=ALIGN))
 
-        def quant(dst, src, cols=slice(0, S)):
+        def quantise(dst, src, cols=slice(0, S)):
             nc.vector.quantize_mx(out=dst[0][:, cols].bitcast(FP8X4), scales=dst[1][:, cols], in_=src[:])
 
-        def mm(dst, lhs, t, rhs, cols=slice(0, S)):
-            m = slice(P * t, P * (t + 1))
-            nc.tensor.matmul_mx(out=dst, lhsT=lhs[0][:, m].bitcast(FP8X4), lhsT_scale=lhs[1][:, m], rhs=rhs[0][:, cols].bitcast(FP8X4), rhs_scale=rhs[1][:, cols], start=True, stop=True)
+        def multiply(dst, lhs, t, rhs, cols=slice(0, S)):
+            rows = slice(P * t, P * (t + 1))
+            nc.tensor.matmul_mx(
+                out=dst,
+                lhsT=lhs[0][:, rows].bitcast(FP8X4),
+                lhsT_scale=lhs[1][:, rows],
+                rhs=rhs[0][:, cols].bitcast(FP8X4),
+                rhs_scale=rhs[1][:, cols],
+                start=True,
+                stop=True,
+            )
 
-        offs_s = pick("offs_s", xs, U8, l_offs)
-        two_s = pick("two_s", xs, U8, l_two)
-        cand_s = pick("cand_s", xs, U8, l_cand)
-        wg1 = keep.tile([P, PACK * S], BF16, name="wg1", align_bytes=64)
-        wg2 = keep.tile([P, PACK * S], BF16, name="wg2", align_bytes=64)
-        weave(wg1, raw1[0], 0)
-        weave(wg1, raw1[1], 1)
-        w1q = codes("w1")
-        quant(w1q, wg1)
-        xq = (pick("offs_w", xw, U32, l_offs), offs_s)
-        xt = (pick("two_w", xw, U32, l_two), two_s)
-        cand_sd = keep.tile([P, S], U8, name="cand_sd", align_bytes=64)
-        nc.vector.tensor_copy(cand_sd[:].rearrange("p (t m) -> p m t", t=PACK), cand_s[:].rearrange("p (m t) -> p m t", t=PACK))
-        w2q = codes("w2")
+        offs_codes = pick("offs_codes", x_codes, U32, l_offs)
+        two_codes = pick("two_codes", x_codes, U32, l_two)
+        offs_bytes = pick("offs_bytes", x_bytes, U8, l_offs)
+        woven1 = keep.tile([P, PACK * S], BF16, name="woven1", align_bytes=ALIGN)
+        woven2 = keep.tile([P, PACK * S], BF16, name="woven2", align_bytes=ALIGN)
+        weave(woven1, raw1[0], 0)
+        weave(woven1, raw1[1], 1)
+        w1_mx = mx_operand("w1")
+        quantise(w1_mx, woven1)
+        two_bytes = pick("two_bytes", x_bytes, U8, l_two)
+        cand_bytes = pick("woven1", x_bytes, U8, l_cand)
+        dealt_bytes = keep.tile([P, S], U8, name="dealt_bytes", align_bytes=ALIGN)
+        nc.vector.tensor_copy(
+            dealt_bytes[:].rearrange("p (t c i) -> p c t i", t=PACK, i=16), cand_bytes[:].rearrange("p (c i t) -> p c t i", t=PACK, i=16)
+        )
+        offs_mx = (offs_codes, offs_bytes)
+        two_mx = (two_codes, two_bytes)
+        w2_mx = mx_operand("w2")
 
-        zg = [keep.tile([P, PACK * HALF], BF16, name="zg%d" % h, align_bytes=64) for h in range(2)]
+        z_woven = [keep.tile([P, PACK * HALF], BF16, name="z_woven%d" % h, align_bytes=ALIGN) for h in range(2)]
+
+        def y_window(t):
+            return windows[(2 * t) % WINDOWS]
+
+        def d_window(t):
+            return windows[(2 * t + 1) % WINDOWS]
+
+        def project(window, acc, weight_mx, t, x_mx):
+            multiply(acc[:], weight_mx, t, x_mx)
+            nc.scalar.copy(window[:, :S], acc[:])
+
+        weave(woven2, raw2[0], 0)
+        project(y_window(0), bank(0), w1_mx, 0, offs_mx)
+        weave(woven2, raw2[1], 1)
+        project(y_window(1), bank(1), w1_mx, 1, offs_mx)
+        quantise(w2_mx, woven2)
+        project(d_window(0), bank(0), w2_mx, 0, two_mx)
+        project(d_window(1), bank(1), w2_mx, 1, two_mx)
         for t in range(PACK):
-            by, bd = bank(t % 2), bank(2 + t % 2)
-            yw, dw = wins[2 * (t % 2)], wins[2 * (t % 2) + 1]
-            if t == 0:
-                weave(wg2, raw2[0], 0)
-            mm(by[:], w1q, t, xq)
-            nc.scalar.copy(yw[:, :S], by[:])
+            if t + 2 < PACK:
+                project(y_window(t + 2), bank(0), w1_mx, t + 2, offs_mx)
+                project(d_window(t + 2), bank(1), w2_mx, t + 2, two_mx)
             if t == 1:
-                g1 = keep.tile([P, S], F32, name="wg2", align_bytes=64)
+                y2 = keep.tile([P, S], F32, name="woven2", align_bytes=ALIGN)
             else:
-                g1 = work.tile([P, S], F32, name="g1")
-            g2 = work.tile([P, S], F32, name="g2")
-            if t < PACK - 1:
-                a = work.tile([P, S], F32, name="a")
+                y2 = work.tile([P, S], F32, name="y2")
+            y1 = work.tile([P, S], F32, name="y1")
+            if t == LAST - 1:
+                first = keep.tile([P, S], F32, name="handover", align_bytes=ALIGN)
             else:
-                a = keep.tile([P, S], F32, name="late", align_bytes=64)
-            b = work.tile([P, S], F32, name="b")
-            m = work.tile([P, S], F32, name="m")
-            nc.vector.tensor_copy(g1[:], yw[:].indirect(l_n1[:]))
-            nc.vector.tensor_copy(g2[:], yw[:].indirect(l_n2[:]))
-            if t == 0:
-                weave(wg2, raw2[1], 1)
-                quant(w2q, wg2)
-            mm(bd[:], w2q, t, xt)
-            nc.scalar.copy(dw[:, :S], bd[:])
-            nc.vector.tensor_tensor(a[:], dw[:].indirect(l_n3[:]), g1[:], ALU.add)
-            nc.vector.tensor_tensor(b[:], dw[:].indirect(l_n4[:]), g2[:], ALU.add)
-            nc.vector.tensor_tensor(m[:], a[:], b[:], ALU.max)
+                first = work.tile([P, S], F32, name="first")
+            if t == LAST:
+                second = keep.tile([P, S], F32, name="handover", align_bytes=ALIGN)
+            else:
+                second = work.tile([P, S], F32, name="second")
+            larger = work.tile([P, S], F32, name="larger")
+            nc.vector.tensor_copy(y2[:], y_window(t)[:].indirect(l_n2[:]))
+            nc.vector.tensor_copy(y1[:], y_window(t)[:].indirect(l_n1[:]))
+            nc.vector.tensor_tensor(second[:], d_window(t)[:].indirect(l_n4[:]), y2[:], ALU.add)
+            nc.vector.tensor_tensor(first[:], d_window(t)[:].indirect(l_n3[:]), y1[:], ALU.add)
+            nc.vector.tensor_tensor(larger[:], first[:], second[:], ALU.max)
             for h in range(2):
-                nc.scalar.activation(zg[h][:].rearrange("p (n t) -> p t n", t=PACK)[:, t, :], m[:, HALF * h : HALF * (h + 1)], ACT.Copy, scale=gs_t[:, t : t + 1])
+                plane = z_woven[h][:].rearrange("p (n t) -> p t n", t=PACK)[:, t, :]
+                nc.scalar.activation(plane, larger[:, HALF * h : HALF * (h + 1)], ACT.Copy, scale=gains[:, t : t + 1])
 
-        cand_w = pick("late", xw, U32, l_cand)
-        cand_wd = keep.tile([P, S], U32, name="cand_wd", align_bytes=64)
-        nc.vector.tensor_copy(cand_wd[:].rearrange("p (t c i) -> p c t i", t=PACK, i=4), cand_w[:].rearrange("p (c i t) -> p c t i", t=PACK, i=4))
-        xc = (cand_wd, cand_sd)
-        zq = codes("z")
+        cand_codes = pick("handover", x_codes, U32, l_cand)
+        dealt_codes = keep.tile([P, S], U32, name="dealt_codes", align_bytes=ALIGN)
+        nc.vector.tensor_copy(
+            dealt_codes[:].rearrange("p (t c i) -> p c t i", t=PACK, i=4), cand_codes[:].rearrange("p (c i t) -> p c t i", t=PACK, i=4)
+        )
+        cand_mx = (dealt_codes, dealt_bytes)
+        z_mx = mx_operand("z")
         for h in range(2):
-            quant(zq, zg[h], slice(HALF * h, HALF * (h + 1)))
+            quantise(z_mx, z_woven[h], slice(HALF * h, HALF * (h + 1)))
 
-        ov = out.rearrange("(p t) n -> t p n", t=PACK)
-        nxs = [keep.tile([P, S], F32, name="nx%d" % t) for t in range(PACK)]
+        out_tiles = out.rearrange("(p t) n -> t p n", t=PACK)
+        shifts = [work.tile([P, S], F32, name="shift", bufs=PACK) for t in range(PACK)]
         for h in range(2):
             cols = slice(HALF * h, HALF * (h + 1))
-            bs = bank(h)
-            mm(bs[:, :HALF], xc, 0, zq, cols)
-            nc.scalar.activation(wins[0][:, cols], bs[:, :HALF], ACT.Copy, scale=0.0625)
-        nc.scalar.activation(nxs[0][:], wins[0][:, :S], ACT.Copy, scale=-5.0 / 3.0)
-        for t in range(1, PACK):
-            bs = bank(t % 2)
-            mm(bs[:], xc, t, zq)
-            nc.scalar.activation(wins[t][:, :S], bs[:], ACT.Copy, scale=0.0625)
-            nc.scalar.activation(nxs[t][:], bs[:], ACT.Copy, scale=-0.0625 * 5.0 / 3.0)
-        pieces = [(t, 0, S) for t in range(PACK - 1)] + [(PACK - 1, 0, HALF), (PACK - 1, HALF, S)]
-        for k, (t, c0, c1) in enumerate(pieces):
-            sp, nx = wins[t], nxs[t]
-            n = c1 - c0
-            lc = slice(c0 // 16, c1 // 16)
-            v = work.tile([P, n], F32, name="g1")
-            ws = work.tile([P, n], F32, name="g2")
-            e = work.tile([P, n], F32, name="a")
-            nn = work.tile([P, n], F32, name="nn", bufs=4)
-            sq1 = work.tile([P, n], F32, name="sq1")
-            sq2 = work.tile([P, n], F32, name="sq2")
-            r = work.tile([P, n], F32, name="r")
-            o = work.tile([P, n], F32, name="o", bufs=4)
-            be, bp, bq = bank(2 + k % 2), bank(4 + k % 2), bank(6 + k % 2)
-            nc.vector.tensor_copy(v[:], sp[:].indirect(l_n6[:, lc]))
-            nc.vector.tensor_tensor(ws[:], sp[:].indirect(l_n5[:, lc]), v[:], ALU.add)
-            turn(bp, (nx[:, c0:c1], ws), n)
-            nc.scalar.activation(sq2[:], bp[:, :n], ACT.Square, scale=0.375 * math.sqrt(0.5))
-            nc.vector.scalar_tensor_tensor(e[:], v[:], -2.0, ws[:], ALU.mult, ALU.add)
-            turn(be, (e,), n)
-            nc.scalar.activation(sq1[:], be[:, :n], ACT.Square, scale=math.sqrt(0.5))
-            nc.vector.scalar_tensor_tensor(nn[:], sp[:, c0:c1], -2.2, ws[:], ALU.mult, ALU.add)
-            turn(bq, (sq2, sq1), n)
-            nc.scalar.activation(r[:], bq[:, :n], ACT.Abs_reciprocal_sqrt, bias=0.25)
-            nc.vector.scalar_tensor_tensor(o[:], nn[:], -0.3125, r[:], ALU.mult, ALU.mult)
-            nc.sync.dma_start(ov[t][:, c0:c1], o[:])
+            acc = bank(h)
+            multiply(acc[:, :HALF], cand_mx, 0, z_mx, cols)
+            nc.scalar.activation(windows[0][:, cols], acc[:, :HALF], ACT.Copy, scale=S_SCALE)
+
+        def scores(t, acc):
+            multiply(acc[:], cand_mx, t, z_mx)
+            nc.scalar.activation(windows[t][:, :S], acc[:], ACT.Copy, scale=S_SCALE)
+
+        def shift(t):
+            nc.scalar.activation(shifts[t][:], windows[t][:, :S], ACT.Copy, scale=-5.0 / 3.0)
+
+        scores(1, bank(7))
+        shift(0)
+        pieces = [(0, 0, HALF), (0, HALF, S)] + [(t, 0, S) for t in range(1, LAST)] + [(LAST, 0, HALF), (LAST, HALF, S)]
+        for index, (t, c0, c1) in enumerate(pieces):
+            if c0 == 0 and t + 1 < PACK:
+                shift(t + 1)
+            if c0 == 0 and t + 2 < PACK:
+                scores(t + 2, bank(t % 2))
+            s_tile = windows[t]
+            width = c1 - c0
+            entries = slice(c0 // 16, c1 // 16)
+            v = work.tile([P, width], F32, name="v")
+            w = work.tile([P, width], F32, name="w")
+            diff = work.tile([P, width], F32, name="diff")
+            centred = work.tile([P, width], F32, name="centred", bufs=6)
+            diff_sq = work.tile([P, width], F32, name="diff_sq", bufs=3)
+            sum_sq = work.tile([P, width], F32, name="sum_sq", bufs=3)
+            inv_root = work.tile([P, width], F32, name="inv_root", bufs=3)
+            result = work.tile([P, width], F32, name="result", bufs=8)
+            nc.vector.tensor_copy(v[:], s_tile[:].indirect(l_n6[:, entries]))
+            nc.vector.tensor_tensor(w[:], s_tile[:].indirect(l_n5[:, entries]), v[:], ALU.add)
+            if index < len(pieces) - 1:
+                diff_acc, sum_acc, var_acc = bank(2 + index % 2), bank(4 + index % 2), bank(6 + index % 2)
+                turn_and_add(sum_acc, (w, shifts[t][:, c0:c1]), width)
+                nc.scalar.activation(sum_sq[:], sum_acc[:, :width], ACT.Square, scale=0.375 * math.sqrt(0.5))
+                nc.vector.scalar_tensor_tensor(diff[:], v[:], -2.0, w[:], ALU.mult, ALU.add)
+                turn_and_add(diff_acc, (diff,), width)
+                nc.scalar.activation(diff_sq[:], diff_acc[:, :width], ACT.Square, scale=math.sqrt(0.5))
+                nc.vector.scalar_tensor_tensor(centred[:], s_tile[:, c0:c1], -2.2, w[:], ALU.mult, ALU.add)
+                turn_and_add(var_acc, (diff_sq, sum_sq), width)
+                nc.scalar.activation(inv_root[:], var_acc[:, :width], ACT.Abs_reciprocal_sqrt, bias=quarter[:])
+            else:
+                total = work.tile([P, width], F32, name="total")
+                var = work.tile([P, width], F32, name="var")
+                nc.vector.scalar_tensor_tensor(diff[:], v[:], -2.0, w[:], ALU.mult, ALU.add)
+                nc.vector.scalar_tensor_tensor(total[:], s_tile[:, c0:c1], -5.0 / 3.0, w[:], ALU.mult, ALU.add)
+                nc.scalar.activation(diff_sq[:], diff[:], ACT.Square, scale=math.sqrt(0.5))
+                nc.scalar.activation(sum_sq[:], total[:], ACT.Square, scale=0.375 * math.sqrt(0.5))
+                nc.vector.scalar_tensor_tensor(centred[:], s_tile[:, c0:c1], -2.2, w[:], ALU.mult, ALU.add)
+                nc.vector.tensor_tensor(var[:], diff_sq[:], sum_sq[:], ALU.add)
+                nc.scalar.activation(inv_root[:], var[:], ACT.Abs_reciprocal_sqrt, bias=quarter[:])
+            nc.vector.scalar_tensor_tensor(result[:], centred[:], -MU, inv_root[:], ALU.mult, ALU.mult)
+            nc.sync.dma_start(out_tiles[t][:, c0:c1], result[:])

import math
from contextlib import ExitStack

import concourse.mybir as mybir
from concourse.masks import make_identity

T = 2048
S = 512
FLOPS = 3 * 2 * S * S * S

F32 = mybir.dt.float32
BF16 = mybir.dt.bfloat16
I32 = mybir.dt.int32
U32 = mybir.dt.uint32
U16 = mybir.dt.uint16
U8 = mybir.dt.uint8
FP8X4 = mybir.dt.float8_e4m3fn_x4
ACT = mybir.ActivationFunctionType
ALU = mybir.AluOpType

P = 128
PACK = 4
HALF = S // 2
ALIGN = 64
WINDOWS = 6
LAST = PACK - 1

S_SCALE = 0.0625
MU = 0.3125


def tile_picked_twcpathbstd_none_p_kernel(tc, x_words, x_scales, w1, w2, gs, offs, two, n1, n2, n3, n4, cand, n5, n6, out):
    nc = tc.nc
    with ExitStack() as ctx:
        lists = ctx.enter_context(tc.tile_pool(name="lists", bufs=1))
        keep = ctx.enter_context(tc.tile_pool(name="keep", bufs=1))
        work = ctx.enter_context(tc.tile_pool(name="work", bufs=2))
        psum = ctx.enter_context(tc.psum_pool(name="psum", bufs=1))

        def load_list(name, src):
            loaded = lists.tile([P, S // 16], U16, name=name)
            nc.sync.dma_start(loaded[:], src)
            return loaded

        def load_half(name, weight, h):
            raw = keep.tile([P, PACK, HALF], F32, name=name)
            nc.sync.dma_start(raw[:], weight.rearrange("(p j) c -> p j c", j=PACK)[:, :, HALF * h : HALF * (h + 1)])
            return raw

        x_bytes = keep.tile([P, T], U8, name="x_bytes", align_bytes=ALIGN)
        nc.vector.memset(x_bytes[:, : T // 2].bitcast(I32), 0)
        nc.gpsimd.memset(x_bytes[:, T // 2 :].bitcast(I32), 0)
        sixteen = keep.tile([P, 1], F32, name="sixteen")
        nc.vector.memset(sixteen[:], 16.0)

        l_offs = load_list("l_offs", offs)
        l_two = load_list("l_two", two)
        x_codes = keep.tile([P, T], U32, name="x_codes", align_bytes=ALIGN)
        nc.sync.dma_start(x_codes[:].bitcast(I32), x_words[0].rearrange("p n t -> p (n t)").bitcast(I32))
        raw1 = [load_half("raw10", w1, 0)]
        for q in range(4):
            nc.sync.dma_start(x_bytes[32 * q : 32 * q + 4, :].bitcast(I32), x_scales[0, 4 * q : 4 * q + 4, :].bitcast(I32))
        raw1.append(load_half("raw11", w1, 1))
        l_cand = load_list("l_cand", cand)
        raw2 = [load_half("raw2%d" % h, w2, h) for h in range(2)]
        l_n1 = load_list("l_n1", n1)
        l_n2 = load_list("l_n2", n2)
        l_n3 = load_list("l_n3", n3)
        l_n4 = load_list("l_n4", n4)
        gains = keep.tile([P, PACK], F32, name="gains")
        nc.sync.dma_start(gains[:], gs.rearrange("(p t) o -> p (t o)", t=PACK))
        l_n5 = load_list("l_n5", n5)
        l_n6 = load_list("l_n6", n6)

        windows = []
        for i in range(WINDOWS):
            window = keep.tile([P, 2 * S], F32, name="window%d" % i)
            nc.vector.memset(window[:, S:], 0.0)
            windows.append(window)
        quarter = keep.tile([P, 1], F32, name="quarter")
        nc.scalar.activation(quarter[:], sixteen[:], ACT.Abs_reciprocal_sqrt)
        ident = keep.tile([P, P], F32, name="ident")
        make_identity(nc, ident[:])

        def bank(i):
            return psum.tile([P, S], F32, name="bank%d" % i)

        def turn_and_add(dst, sources, width):
            for c in range(width // P):
                block = slice(P * c, P * (c + 1))
                for i, src in enumerate(sources):
                    nc.tensor.matmul(dst[:, block], src[:, block], ident[:], start=(i == 0), stop=(i == len(sources) - 1), is_transpose=True)

        def pick(tag, table, dtype, offsets):
            picked = keep.tile([P, S], dtype, name=tag, align_bytes=ALIGN)
            nc.vector.tensor_copy(picked[:], table[:].indirect(offsets[:]))
            return picked

        def weave(woven, raw, h):
            dealt = woven[:].rearrange("p (t m j) -> p m t j", t=PACK, j=PACK)
            per_half = HALF // PACK
            nc.scalar.copy(dealt[:, per_half * h : per_half * (h + 1)], raw[:].rearrange("p j (m t) -> p m t j", t=PACK))

        def mx_operand(name):
            return (keep.tile([P, S], U32, name=name + "_codes", align_bytes=ALIGN), keep.tile([P, S], U8, name=name + "_bytes", align_bytes=ALIGN))

        def quantise(dst, src, cols=slice(0, S)):
            nc.vector.quantize_mx(out=dst[0][:, cols].bitcast(FP8X4), scales=dst[1][:, cols], in_=src[:])

        def multiply(dst, lhs, t, rhs, cols=slice(0, S)):
            rows = slice(P * t, P * (t + 1))
            nc.tensor.matmul_mx(
                out=dst,
                lhsT=lhs[0][:, rows].bitcast(FP8X4),
                lhsT_scale=lhs[1][:, rows],
                rhs=rhs[0][:, cols].bitcast(FP8X4),
                rhs_scale=rhs[1][:, cols],
                start=True,
                stop=True,
            )

        offs_codes = pick("offs_codes", x_codes, U32, l_offs)
        two_codes = pick("two_codes", x_codes, U32, l_two)
        offs_bytes = pick("offs_bytes", x_bytes, U8, l_offs)
        woven1 = keep.tile([P, PACK * S], BF16, name="woven1", align_bytes=ALIGN)
        woven2 = keep.tile([P, PACK * S], BF16, name="woven2", align_bytes=ALIGN)
        weave(woven1, raw1[0], 0)
        weave(woven1, raw1[1], 1)
        w1_mx = mx_operand("w1")
        quantise(w1_mx, woven1)
        two_bytes = pick("two_bytes", x_bytes, U8, l_two)
        cand_bytes = pick("woven1", x_bytes, U8, l_cand)
        dealt_bytes = keep.tile([P, S], U8, name="dealt_bytes", align_bytes=ALIGN)
        nc.vector.tensor_copy(
            dealt_bytes[:].rearrange("p (t c i) -> p c t i", t=PACK, i=16), cand_bytes[:].rearrange("p (c i t) -> p c t i", t=PACK, i=16)
        )
        offs_mx = (offs_codes, offs_bytes)
        two_mx = (two_codes, two_bytes)
        w2_mx = mx_operand("w2")

        z_woven = [keep.tile([P, PACK * HALF], BF16, name="z_woven%d" % h, align_bytes=ALIGN) for h in range(2)]

        def y_window(t):
            return windows[(2 * t) % WINDOWS]

        def d_window(t):
            return windows[(2 * t + 1) % WINDOWS]

        def project(window, acc, weight_mx, t, x_mx):
            multiply(acc[:], weight_mx, t, x_mx)
            nc.scalar.copy(window[:, :S], acc[:])

        weave(woven2, raw2[0], 0)
        project(y_window(0), bank(0), w1_mx, 0, offs_mx)
        weave(woven2, raw2[1], 1)
        project(y_window(1), bank(1), w1_mx, 1, offs_mx)
        quantise(w2_mx, woven2)
        project(d_window(0), bank(0), w2_mx, 0, two_mx)
        project(d_window(1), bank(1), w2_mx, 1, two_mx)
        for t in range(PACK):
            if t + 2 < PACK:
                project(y_window(t + 2), bank(0), w1_mx, t + 2, offs_mx)
                project(d_window(t + 2), bank(1), w2_mx, t + 2, two_mx)
            if t == 1:
                y2 = keep.tile([P, S], F32, name="woven2", align_bytes=ALIGN)
            else:
                y2 = work.tile([P, S], F32, name="y2")
            y1 = work.tile([P, S], F32, name="y1")
            if t == LAST - 1:
                first = keep.tile([P, S], F32, name="handover", align_bytes=ALIGN)
            else:
                first = work.tile([P, S], F32, name="first")
            if t == LAST:
                second = keep.tile([P, S], F32, name="handover", align_bytes=ALIGN)
            else:
                second = work.tile([P, S], F32, name="second")
            larger = work.tile([P, S], F32, name="larger")
            nc.vector.tensor_copy(y2[:], y_window(t)[:].indirect(l_n2[:]))
            nc.vector.tensor_copy(y1[:], y_window(t)[:].indirect(l_n1[:]))
            nc.vector.tensor_tensor(second[:], d_window(t)[:].indirect(l_n4[:]), y2[:], ALU.add)
            nc.vector.tensor_tensor(first[:], d_window(t)[:].indirect(l_n3[:]), y1[:], ALU.add)
            nc.vector.tensor_tensor(larger[:], first[:], second[:], ALU.max)
            for h in range(2):
                plane = z_woven[h][:].rearrange("p (n t) -> p t n", t=PACK)[:, t, :]
                nc.scalar.activation(plane, larger[:, HALF * h : HALF * (h + 1)], ACT.Copy, scale=gains[:, t : t + 1])

        cand_codes = pick("handover", x_codes, U32, l_cand)
        dealt_codes = keep.tile([P, S], U32, name="dealt_codes", align_bytes=ALIGN)
        nc.vector.tensor_copy(
            dealt_codes[:].rearrange("p (t c i) -> p c t i", t=PACK, i=4), cand_codes[:].rearrange("p (c i t) -> p c t i", t=PACK, i=4)
        )
        cand_mx = (dealt_codes, dealt_bytes)
        z_mx = mx_operand("z")
        for h in range(2):
            quantise(z_mx, z_woven[h], slice(HALF * h, HALF * (h + 1)))

        out_tiles = out.rearrange("(p t) n -> t p n", t=PACK)
        shifts = [work.tile([P, S], F32, name="shift", bufs=PACK) for t in range(PACK)]
        for h in range(2):
            cols = slice(HALF * h, HALF * (h + 1))
            acc = bank(h)
            multiply(acc[:, :HALF], cand_mx, 0, z_mx, cols)
            nc.scalar.activation(windows[0][:, cols], acc[:, :HALF], ACT.Copy, scale=S_SCALE)

        def scores(t, acc):
            multiply(acc[:], cand_mx, t, z_mx)
            nc.scalar.activation(windows[t][:, :S], acc[:], ACT.Copy, scale=S_SCALE)

        def shift(t):
            nc.scalar.activation(shifts[t][:], windows[t][:, :S], ACT.Copy, scale=-5.0 / 3.0)

        scores(1, bank(7))
        shift(0)
        pieces = [(0, 0, HALF), (0, HALF, S)] + [(t, 0, S) for t in range(1, LAST)] + [(LAST, 0, HALF), (LAST, HALF, S)]
        for index, (t, c0, c1) in enumerate(pieces):
            if c0 == 0 and t + 1 < PACK:
                shift(t + 1)
            if c0 == 0 and t + 2 < PACK:
                scores(t + 2, bank(t % 2))
            s_tile = windows[t]
            width = c1 - c0
            entries = slice(c0 // 16, c1 // 16)
            v = work.tile([P, width], F32, name="v")
            w = work.tile([P, width], F32, name="w")
            diff = work.tile([P, width], F32, name="diff")
            centred = work.tile([P, width], F32, name="centred", bufs=6)
            diff_sq = work.tile([P, width], F32, name="diff_sq", bufs=3)
            sum_sq = work.tile([P, width], F32, name="sum_sq", bufs=3)
            inv_root = work.tile([P, width], F32, name="inv_root", bufs=3)
            result = work.tile([P, width], F32, name="result", bufs=8)
            nc.vector.tensor_copy(v[:], s_tile[:].indirect(l_n6[:, entries]))
            nc.vector.tensor_tensor(w[:], s_tile[:].indirect(l_n5[:, entries]), v[:], ALU.add)
            if index < len(pieces) - 1:
                diff_acc, sum_acc, var_acc = bank(2 + index % 2), bank(4 + index % 2), bank(6 + index % 2)
                turn_and_add(sum_acc, (w, shifts[t][:, c0:c1]), width)
                nc.scalar.activation(sum_sq[:], sum_acc[:, :width], ACT.Square, scale=0.375 * math.sqrt(0.5))
                nc.vector.scalar_tensor_tensor(diff[:], v[:], -2.0, w[:], ALU.mult, ALU.add)
                turn_and_add(diff_acc, (diff,), width)
                nc.scalar.activation(diff_sq[:], diff_acc[:, :width], ACT.Square, scale=math.sqrt(0.5))
                nc.vector.scalar_tensor_tensor(centred[:], s_tile[:, c0:c1], -2.2, w[:], ALU.mult, ALU.add)
                turn_and_add(var_acc, (diff_sq, sum_sq), width)
                nc.scalar.activation(inv_root[:], var_acc[:, :width], ACT.Abs_reciprocal_sqrt, bias=quarter[:])
            else:
                total = work.tile([P, width], F32, name="total")
                var = work.tile([P, width], F32, name="var")
                nc.vector.scalar_tensor_tensor(diff[:], v[:], -2.0, w[:], ALU.mult, ALU.add)
                nc.vector.scalar_tensor_tensor(total[:], s_tile[:, c0:c1], -5.0 / 3.0, w[:], ALU.mult, ALU.add)
                nc.scalar.activation(diff_sq[:], diff[:], ACT.Square, scale=math.sqrt(0.5))
                nc.scalar.activation(sum_sq[:], total[:], ACT.Square, scale=0.375 * math.sqrt(0.5))
                nc.vector.scalar_tensor_tensor(centred[:], s_tile[:, c0:c1], -2.2, w[:], ALU.mult, ALU.add)
                nc.vector.tensor_tensor(var[:], diff_sq[:], sum_sq[:], ALU.add)
                nc.scalar.activation(inv_root[:], var[:], ACT.Abs_reciprocal_sqrt, bias=quarter[:])
            nc.vector.scalar_tensor_tensor(result[:], centred[:], -MU, inv_root[:], ALU.mult, ALU.mult)
            nc.sync.dma_start(out_tiles[t][:, c0:c1], result[:])
